import numpy as np, ml_dtypes
CORES = [40,64,80,88,96,104,120,144]
N = 8
import mx_ref
BF = ml_dtypes.bfloat16
def gentries(a):
    return np.ascontiguousarray(a.reshape(8, 16, -1).transpose(0, 2, 1)).reshape(8, -1)
def gtable(e):
    e = np.asarray(e); return np.ascontiguousarray(e.reshape(8, -1, 16).transpose(0, 2, 1)).reshape(128, -1).astype(np.int32)
def gcols(t, e):
    v = np.concatenate([t.reshape(8, 16, -1, 4), np.zeros((8, 16, 1, 4), BF)], axis=2)
    return np.ascontiguousarray(np.stack([v[g][:, e[g]] for g in range(8)])).reshape(128, -1)
def gpick(z, e):
    return np.concatenate([z[16 * g:16 * g + 16][:, e[g]] for g in range(8)])
def tile(rs):
    return np.stack(rs, axis=2).reshape(128, -1).astype(BF)
def pick(q, e):
    c = np.concatenate([q[0].reshape(128, -1, 4), np.zeros((128, 1, 4), np.uint8)], axis=1); s = np.concatenate([q[1], np.ones((16, 1), np.uint8)], axis=1)
    return (np.ascontiguousarray(c[:, e].reshape(128, -1)), np.ascontiguousarray(s[:, e]))
def join(*qs):
    return (np.concatenate([q[0] for q in qs], axis=1), np.concatenate([q[1] for q in qs], axis=1))
def put(q, e, v):
    c, s = q[0].reshape(128, -1, 4).copy(), q[1].copy(); c[:, e] = v[0].reshape(128, -1, 4); s[:, e] = v[1]
    return (c.reshape(128, -1), s)
def pk(c, s):
    return (np.ascontiguousarray(c), mx_ref.live(s))
def emit(q):
    return q[0], q[1]
def packed(v, rng):
    q = [mx_ref.quantize(np.ascontiguousarray(v[r])) for r in range(N)]
    return np.stack([a for a, b in q]), np.stack([mx_ref.plane(b, rng) for a, b in q])
def values_of_codes():
    e, c = np.zeros((128, 128, 4), np.float32), np.zeros((128, 2, 4), np.uint8)
    e[np.arange(128), np.arange(128), 0] = 1
    c[:127, :, 0] = np.arange(256).reshape(2, 128).T[:127]
    return mx_ref.matmul(mx_ref.quantize(e.reshape(128, 512).astype(BF)), (c.reshape(128, 8), np.full((16, 2), 127, np.uint8))).T.reshape(-1).astype(np.float64)
CODE_VALUE, SCALE_VALUE = values_of_codes(), 2.0 ** (np.arange(256) - 127.0)
def decode(q):
    return (CODE_VALUE[q[0]].reshape(16, 8, -1, 4) * SCALE_VALUE[q[1]][:, None, :, None] + 0.0).reshape(128, -1).astype(np.float32)
def f(rng, *shape):
    return mx_ref.flush((rng.standard_normal(shape, dtype=np.float32) * np.exp2(rng.integers(-2, 3, shape[:-1] + (1,)))).astype(BF))
def wide(rng, *shape, cols=0):
    v = rng.standard_normal(shape, dtype=np.float32) * np.exp2(rng.integers(-12, 13, shape)).astype(np.float32)
    if cols: v *= np.repeat(np.exp2(rng.integers(-cols, cols + 1, shape[:-2] + (1, shape[-1] // 4))) * (rng.random(shape[:-2] + (1, shape[-1] // 4)) > 0.0625), 4, axis=-1).astype(np.float32)
    return mx_ref.flush(v.astype(BF))
C = 288
STEP = [4, 1, 2]
def numbers_of(rng):
    return {"x": np.array(f(rng, N, 128, 4 * C)), "u": np.array(f(rng, N, 128, 512)), "v": np.array(f(rng, N, 128, 512))}
def stored(k):
    return {"od": np.stack([gtable(k[r]) for r in range(N)])}
def orders(rng):
    return stored(rng.permuted(np.tile(np.arange(C), (N, 8, 1)), axis=2))
def rings(rng):
    h = rng.permutation(8)
    pairs = [1] + [2] * (C // 2 - 1) + [1]
    sizes = [[C], [C], [1, C - 1], [257, C - 257], pairs, pairs, [C // 2, C // 2], [1] * C]
    i = np.arange(N)
    odd = (i ^ (i >> 1) ^ (i >> 2)) % 2
    k = np.zeros((N, 8, C), np.int64)
    for g in range(8):
        w = np.arange(C) if h[g] % 2 == 0 else rng.permutation(C)
        c, after = rng.permutation(C), np.zeros(C, np.int64)
        a = 0
        for m in sizes[h[g]]:
            after[w[a:a + m]] = np.roll(w[a:a + m], -1)
            a += m
        k[:, g] = np.where(odd[:, None] == 1, c[after], c)
    return stored(k)
def layers(rng):
    return np.array(f(rng, N, 128, 2048)).reshape(N, 8, 16, 4, 8, 16, 4)
def weights(rng, w):
    c, s = packed(np.ascontiguousarray(w).reshape(N, 128, 2048), rng)
    return {"wc": c, "ws": s}
def setup_inputs(rng):
    return {**numbers_of(rng), **orders(rng), **weights(rng, layers(rng))}
def setup_inputs_ties(rng):
    d = numbers_of(rng)
    o = rng.permutation(N)
    k = rng.integers(-1, 2, (N, 8, C)).astype(np.float32)
    k[o[0]] = 0
    k[o[1]] = 1
    k[o[2]] = -1
    x = d["x"].reshape(N, 8, 16, C, 4)
    x[:, :, 0] = 0
    x[:, :, 0, :, 0] = k.astype(BF)
    u = d["u"].reshape(N, 128, 128, 4)
    u[:, :, ::16] = 0
    for h in range(0, 128, 16): u[:, h, h, 0] = 1
    w = layers(rng)
    w[:, :, :, :, :, 0] = 0
    return {"x": x.reshape(N, 128, 4 * C), "u": u.reshape(N, 128, 512), "v": d["v"], **rings(rng), **weights(rng, w)}
def setup_inputs_near(rng):
    d = numbers_of(rng)
    small = ((np.arange(N) & STEP[1]) > 0) ^ (rng.random() < 0.5)
    k = np.where(small, 2.0 ** -30, 1.0)
    x = d["x"].astype(np.float32).reshape(N, 8, 16, C, 4)
    x[:, :, :8] = 0
    s = rng.integers(-1, 2, (N, 8, C)) * k[:, None, None]
    x[:, :, 0, :, 0] = 1.125 * s
    x[:, :, 1, :, 0] = -1.25 * s
    x[:, :, 2, :, 0] = rng.choice([-1.0, 1.0], (N, 8, C)) * 2.0 ** -30
    x[:, :, 4, :, 0] = 2.0 ** -30
    for r in range(N):
        at = [0, C - 1, int(rng.integers(C)), int(rng.integers(C))]
        for g, j in zip(rng.permutation(8)[:4], at): x[r, g, 0, j, 0] = 2.0 ** 30 * rng.choice([-1.0, 1.0])
    k = k.astype(np.float32)
    u = d["u"].reshape(N, 128, 128, 4)
    u[:, :, ::16] = 0
    for h in range(0, 128, 16):
        u[:, h, h, 0] = (1.125 * k).astype(BF)
        u[:, h + 1, h, 0] = k.astype(BF)
        u[:, h + 3, h, 0] = k.astype(BF)
    w = layers(rng)
    w[:, :, :8] = 0
    w[:, :, :, :, :, :8] = 0
    for r in range(N):
        for g in range(8):
            if small[r]: w[r, g, 2, 0, g, 3, 0] = 2.0 ** -8
    return {"x": x.reshape(N, 128, 4 * C).astype(BF), "u": u.reshape(N, 128, 512), "v": d["v"], **orders(rng), **weights(rng, w)}
def setup_inputs_odd(rng):
    d = numbers_of(rng)
    x = (1.0 + (2 * rng.integers(0, 64, (N, 16, 8, C, 4)) + 1) * 2.0 ** -7) * np.exp2(-rng.integers(0, 7, (N, 16, 8, C, 4)).astype(np.float64)) * rng.choice([-1.0, 1.0], (N, 16, 8, C, 4))
    x[:, :, 0, :, 0] = np.where(rng.random((N, 16, C)) < 0.5, 1.96875, 1.875) * 2.0 ** 8 * rng.choice([-1.0, 1.0], (N, 16, 1))
    x[:, ::2, 1, :, 0] = rng.integers(7, 10, (N, 8, C)) * 2.0 ** -8
    x[:, ::2, 2, :, 0] = -8 * 2.0 ** -8
    u = d["u"].reshape(N, 16, 8, 128, 4)
    u[:, :, :, ::16] = 0
    for g in range(8): u[:, 2 * g, 1:3, 16 * g, 0] = 1
    w = layers(rng)
    for i in (0, 8):
        w[:, :, i] = 0
        w[:, :, :, :, :, i] = 0
    return {"x": x.astype(np.float32).reshape(N, 128, 4 * C).astype(BF), "u": u.reshape(N, 128, 512), "v": d["v"], **orders(rng), **weights(rng, w)}
def setup_inputs_ends(rng):
    d = numbers_of(rng)
    o, most = rng.permutation(N) % 4, rng.permutation(N) % 2
    h, e = rng.permutation(8), int(rng.integers(8))
    c = np.where(h < 2, 0.0, h % 2 * 2.0 - 1.0)[None, :, None]
    k = np.array([2.0, 4.0])[rng.permutation(8) % 2]
    x = np.zeros((N, 8, 16, C, 4))
    u = d["u"].astype(np.float32).reshape(N, 128, 128, 4)
    v = np.zeros((N, 128, 512), np.float32)
    w = np.zeros((N, 128, 4, 128, 4), np.float32)
    i = np.arange(128)
    for r in range(N):
        low = -0.7 * (0.9 + 0.1 * rng.random((8, 16, C, 4))) * 2.0 ** 30
        tiny = -(1.0 + 0.125 * rng.integers(0, 8, (8, 16, C, 4))) * 2.0 ** -30
        if o[r] == 0: x[r] = low
        if o[r] == 1: x[r] = np.where((rng.random(C) < 0.5)[:, None], 0.7 * (1.0 + 0.4 * rng.random((8, 16, C, 4))) * 2.0 ** 27, low)
        if o[r] == 2: x[r] = tiny
        if o[r] == 3: x[r] = d["x"][r].astype(np.float32).reshape(8, 16, C, 4)[:, :, :1]
        x[r, e, 8:] = tiny[e, 8:, :1] if o[r] == 3 else tiny[e, 8:]
        if o[r] < 2: u[r, :, ::16] = c * (0.9 + 0.1 * rng.random((128, 8, 4))) * 2.0 ** 30
        if o[r] == 2: u[r, :, ::16] = c * (1.0 + 0.125 * rng.integers(0, 8, (128, 8, 4))) * 2.0 ** -30
        if o[r] == 3: u[r, :, ::16] *= np.abs(c).astype(np.float32)
        a = (0.9 + 0.1 * rng.random((128, 512))) * 2.0 ** 30 if o[r] < 2 else (1.0 + 0.125 * rng.integers(0, 8, (128, 512))) * 2.0 ** -30
        v[r] = rng.choice([-1.0, 1.0], (128, 512)) * a
        t = k[i // 16]
        t[16 * e + 8:16 * e + 16] = 2.0 ** 8 if most[r] else 2.0 ** -8
        for b in range(4): w[r, i, b, i, b] = t
    return {"x": x.astype(np.float32).reshape(N, 128, 4 * C).astype(BF), "u": u.reshape(N, 128, 512).astype(BF), "v": v.astype(BF), **rings(rng), **weights(rng, w.astype(BF))}
def setup_inputs_spread(rng):
    d = setup_inputs(rng)
    d["x"] = wide(rng, N, 128, 4 * C, cols=6)
    return d
def check_inputs(d):
    b = []
    for k in ("x", "u", "v"):
        a = np.abs(d[k].astype(np.float32))
        if not (np.isfinite(a).all() and ((a == 0) | (a >= 2.0 ** -30) & (a <= 2.0 ** 30)).all()): b.append("a value of " + k)
    none, least, most = [emit(mx_ref.quantize(np.full((128, 16), k, np.float32).astype(BF)))[1][0, 0] for k in (0.0, 2.0 ** -8, 2.0 ** 8)]
    for r in range(N):
        if not (np.sort(gentries(d["od"][r]), axis=1) == np.arange(C)).all(): b.append("od: a group whose entries are not all columns once")
        if ((d["wc"][r] == 0x7F) | (d["wc"][r] == 0xFF)).any(): b.append("wc: a code that is no number")
        s = mx_ref.live(d["ws"][r])
        if ((s != none) & ((s < least) | (s > most))).any(): b.append("ws: a scale out of range")
        if (((d["wc"][r].reshape(16, 8, 512, 4) & 0x7F) != 0) & (s == none)[:, None, :, None]).any(): b.append("wc: a code other than zero under the scale of zeros")
    return b
def at(t, e):
    return np.take_along_axis(t, e, axis=1)
def reference(x, u, v, od, wc, ws):
    qu = [mx_ref.quantize(u[r]) for r in range(N)]
    lay = [pk(wc[r], ws[r]) for r in range(N)]
    now = [x[r] for r in range(N)]
    order = [gentries(od[r]).astype(np.int64) for r in range(N)]
    for step in STEP:
        old, order, far, z = order, [], [], []
        for r in range(N):
            q = mx_ref.quantize(now[r])
            s = mx_ref.matmul(qu[r], q)[::16]
            mine, other = old[r], old[r ^ step]
            jump = at(np.argsort(other, axis=1), mine)
            low = np.tile(np.arange(C), (8, 1))
            for i in range(9):
                low = np.minimum(low, at(low, jump))
                jump = at(jump, jump)
            order.append(np.where(at(s, at(mine, low)) > 0, other, mine))
            far.append(decode(q))
            t = far[r].astype(BF)
            pair = gcols(t, order[r]).astype(np.float32) + gcols(t, at(order[r], order[r])).astype(np.float32)
            z.append(mx_ref.quantize((pair * np.float32(0.5)).astype(BF)))
        for r in range(N):
            back = np.argsort(order[r], axis=1)
            now[r] = tile([gpick(mx_ref.matmul(pick(lay[r], np.arange(128 * b, 128 * b + 128)), z[r ^ step]) * np.float32(0.03125), back) + far[r][:, b::4] for b in range(4)])
    y, fo = np.zeros((N, 128, C), np.float32), np.zeros((N, 8, C), np.float32)
    oc, osc = np.zeros((N, 128, 4 * C), np.uint8), np.zeros((N, 16, C), np.uint8)
    for r in range(N):
        q = mx_ref.quantize(now[r])
        y[r] = mx_ref.matmul(mx_ref.quantize(v[r]), q)
        fo[r] = order[r]
        oc[r], osc[r] = emit(q)
    return {"y": y, "fo": fo, "oc": oc, "osc": osc}

@@ -1,0 +1,377 @@
+from concourse.bass import DstId, RemoteDMATransfer
+from concourse.mybir import dt, AluOpType, ActivationFunctionType
+
+C = 288
+STEP = [4, 1, 2]
+RAD = [2, 2, 2, 2, 2, 3, 3]
+MID = 4
+F32, BF, I32, U16, U8, MX = "float32", "bfloat16", "int32", "uint16", "uint8", "float8_e4m3fn_x4"
+
+
+def _scratch():
+    s = {}
+
+    def sb(dtype, **names):
+        for k in names: s[k] = ("sbuf", [128, names[k]], dtype)
+    sb(I32, odi=18, bi=18, hod=18, pidx=1, p15=1, zki=36, zkm=36)
+    sb(U16, ofc=36, uof=8, b0=18, bv=18, hiv=18, ll=36)
+    for k in range(4): sb(U16, **{"aw%d" % k: 36})
+    for k in (1, 2): sb(U16, **{"hw%d" % k: 36, "bw%d" % k: 36})
+    for k in range(len(RAD)): sb(U16, **{"lo%d" % k: 18})
+    sb(BF, xin=4 * C, uin=512, vin=512, et=2048, zt=4 * C, xt=4 * C)
+    sb(BF, ci=C, scc=2 * C, ivr=C, ja=C, jb=C, jc=C, zj=C, fl=C, tf=2 * C, zf=2 * C)
+    for k in (1, 2): sb(BF, **{"op%d" % k: C})
+    sb(F32, iot=512, i5=C, p4=4, p16=1, sct=1, scol=1, ne=16, nx=16, t1=16, t2=16, sc16=16, dk16=16, dkk=2 * C)
+    sb(F32, k0=C, k1=C, k2=C, c0=C, c1=C, gs=4 * C, kk=2 * C, zk=2 * C, bf=36, df=36, fw=36, fm=36, af0=36, af1=36, af2=36, af3=36)
+    sb(F32, fs=4 * C, ys=4 * C, fp=4 * C, rr=4 * C, yo=C, fr=C)
+    for k, n in (("w", 512), ("e", 512), ("u", 128), ("ur", 128), ("v", 128)): sb(MX, **{k + "q": n}); sb(U8, **{k + "p": n})
+    for k in range(4): sb(MX, **{"xq%d" % k: C}); sb(U8, **{"xs%d" % k: C})
+    for k in range(3):
+        for a in "zhr": sb(MX, **{"%sq%d" % (a, k): C}); sb(U8, **{"%ss%d" % (a, k): C})
+    s["pd"] = ("psum", [128, 2048], F32)
+    s["pr"] = ("psum", [128, 2048], F32)
+    return s
+
+
+SCRATCH = _scratch()
+SEMAPHORES = ["cv", "cs", "ct", "cg", "lod", "lx", "lu", "lv", "lwc", "lws", "store", "sent",
+              "hod", "hiv", "hw1", "hw2", "hq0", "hq1", "hq2", "hs0", "hs1", "hs2",
+              "roda", "rodc", "riv", "rw1", "rw2", "rqa0", "rqa1", "rqa2", "rqb0", "rqb1", "rqb2", "rs0", "rs1", "rs2"]
+
+
+def _mask(es):
+    return sum(1 << e for e in es)
+
+
+def _helpers(rc, dest, topo):
+    h = [c for c in topo.cores_of(rc) if c != rc and topo.may_write(c, dest)]
+    near = [c for c in h if topo.die(c) == topo.die(rc)]
+    far = [c for c in h if topo.die(c) != topo.die(rc)]
+    return near[0], far[0], near[1]
+
+
+def _relay(g, core, rc, T, topo):
+    rank, n = T.rank_of(rc), 0
+
+    def fwd(dest, dst, src, sem):
+        rid, pid = topo.addr(dest, core)
+        g.remote_dma(out_ap=dst, in_ap=src, remote_sem=T.sem[sem], local_sem=T.sem["sent"], pid=pid, routing_id=rid, dma_engine_mask=topo.mask(core, dest))
+        return len(topo.engines(core, dest))
+
+    def on_chip(k):
+        return len(topo.engines(rc, core)) // k
+    dests = [T.cores[rank ^ s] for s in STEP]
+    for t, dest in enumerate(dests):
+        a, b, c = _helpers(rc, dest, topo)
+        if t == 0:
+            for h, lo, sem in ((a, 0, "roda"), (c, 9, "rodc")):
+                if core == h:
+                    g.wait_ge(T.sem["hod"], on_chip(4))
+                    n += fwd(dest, T["bi"][:, lo:lo + 9], T["hod"][:, lo:lo + 9], sem)
+            if core == b:
+                g.wait_ge(T.sem["hiv"], on_chip(2))
+                n += fwd(dest, T["bv"][:, :], T["hiv"][:, :], "riv")
+        if t < 2 and core == _helpers(rc, dests[t + 1], topo)[0]:
+            k = "w%d" % (t + 1)
+            g.wait_ge(T.sem["h" + k], on_chip(2))
+            n += fwd(dests[t + 1], T["b" + k][:, :], T["h" + k][:, :], "r" + k)
+        for h, lo, sem in ((a, 0, "rqa"), (b, C // 2, "rqb")):
+            if core == h:
+                k = "q%d" % t
+                g.wait_ge(T.sem["h" + k], on_chip(2))
+                n += fwd(dest, T["r" + k][:, lo:lo + C // 2].bitcast(dt.uint8), T["h" + k][:, lo:lo + C // 2].bitcast(dt.uint8), "%s%d" % (sem, t))
+        if core == c:
+            k = "s%d" % t
+            g.wait_ge(T.sem["h" + k], on_chip(1))
+            n += fwd(dest, T["r" + k][:, :], T["h" + k][:, :], "r" + k)
+    if n: g.wait_ge(T.sem["sent"], n)
+
+
+def rank_program(g, core, T, topo):
+    rank = T.rank_of(core)
+    if rank is None:
+        for c in topo.cores_of(core):
+            if T.rank_of(c) is not None: _relay(g, core, c, T, topo)
+        return
+    A = AluOpType
+    COPY = ActivationFunctionType.Copy
+    eng = {"v": g.vector, "s": g.scalar, "t": g.tensor, "y": g.sync, "g": g}
+    count, last_write, readers = {}, {}, {}
+    known = {q: {} for q in eng}
+
+    def settle(q, events):
+        best = {}
+        for s, n, snap in events:
+            if known[q].get(s, 0) < n and (s not in best or best[s][0] < n): best[s] = (n, snap)
+        for s in list(best):
+            if any(o != s and best[o][1].get(s, 0) >= best[s][0] for o in best): del best[s]
+        for s in best:
+            n, snap = best[s]
+            eng[q].wait_ge(T.sem[s], n)
+            for k, m in list(snap.items()) + [(s, n)]: known[q][k] = max(known[q].get(k, 0), m)
+
+    def call(q, make, reads, writes, sem=None, step=1):
+        banks = [r for r in reads if r[:2] in ("pd", "pr")]
+        events = []
+        for r in reads: events += last_write.get(r, [])
+        for r in writes + banks: events += last_write.get(r, []) + readers.get(r, [])
+        settle(q, events)
+        ins = make(eng[q])
+        s = sem or "c" + q
+        count[s] = count.get(s, 0) + step
+        ins.then_inc(T.sem[s], step)
+        e = (s, count[s], dict(known[q]))
+        for r in reads: readers.setdefault(r, []).append(e)
+        for r in writes: last_write[r], readers[r] = [e], []
+
+    def arrived(regions, *events):
+        for r in regions: last_write[r], readers[r] = [(s, n, {}) for s, n in events], []
+
+    def load(q, dst, src, sem, writes): call(q, lambda e: e.dma_start(dst, src), [], writes, sem, 16)
+
+    def store(q, dst, src, reads): call(q, lambda e: e.dma_start(dst, src), reads, [], "store", 16)
+
+    def tt(out, in0, in1, op, reads, writes): call("v", lambda e: e.tensor_tensor(out, in0, in1, op), reads, writes)
+
+    def ts(out, in0, s1, s2, op0, op1, reads, writes):
+        if op1 is None: call("v", lambda e: e.tensor_scalar(out, in0, s1, None, op0), reads, writes)
+        else: call("v", lambda e: e.tensor_scalar(out, in0, s1, s2, op0, op1), reads, writes)
+
+    def vcopy(out, in_, reads, writes): call("v", lambda e: e.tensor_copy(out, in_), reads, writes)
+
+    def scopy(out, in_, reads, writes, scale=1.0):
+        if scale == 1.0: call("s", lambda e: e.activation(out, in_, COPY), reads, writes)
+        else: call("s", lambda e: e.activation(out, in_, COPY, scale=scale), reads, writes)
+
+    def scan(out, d0, d1, op0, op1, reads, writes): call("v", lambda e: e.tensor_tensor_scan(out, d0, d1, 0.0, op0, op1), reads, writes)
+
+    def quant(q, s, in_, reads, writes): call("v", lambda e: e.quantize_mx(q, s, in_), reads, writes)
+
+    def mm(out, lq, ls, rq, rs, reads, writes): call("t", lambda e: e.matmul_mx(out, lq, ls, rq, rs, True, True), reads, writes)
+
+    sent = [0]
+    dests = [T.cores[rank ^ s] for s in STEP]
+    back = [[len(topo.engines(h, core)) for h in _helpers(d, core, topo)] for d in dests]
+
+    def send(reads, *parts):
+        settle("g", [e for r in reads for e in last_write.get(r, [])])
+        if len(parts) == 1:
+            h, dst, src, sem, es = parts[0]
+            rid, pid = topo.addr(h, core)
+            g.remote_dma(out_ap=dst, in_ap=src, remote_sem=T.sem[sem], local_sem=T.sem["sent"], pid=pid, routing_id=rid, dma_engine_mask=_mask(es))
+        else:
+            moves = []
+            for h, dst, src, sem, es in parts:
+                rid, pid = topo.addr(h, core)
+                moves.append(RemoteDMATransfer(dst_ids=[DstId(rid=rid, pnc=pid)], dma_engine_mask=_mask(es), remote_sem=T.sem[sem], src=src, dst=dst))
+            g.remote_dma_fused(moves, local_sem=T.sem["sent"])
+        sent[0] += sum(len(p[4]) for p in parts)
+
+    load("y", T["odi"][:, :], T.od[:, :], "lod", ["odi"])
+    load("s", T["xin"][:, :], T.x[:, :], "lx", ["xin"])
+    load("y", T["uin"][:, :], T.u[:, :], "lu", ["uin"])
+    load("y", T["wq"][:, :].bitcast(dt.uint8), T.wc[:, :], "lwc", ["wq"])
+    load("y", T["wp"][:, :], T.ws[:, :], "lws", ["wp"])
+    load("y", T["vin"][:, :], T.v[:, :], "lv", ["vin"])
+    ha, hb, hc = _helpers(core, dests[0], topo)
+    es = topo.engines(core, ha)
+    iot, ci = T["iot"], T["ci"]
+    call("g", lambda e: e.iota(iot[:, :], [[1, 512]], 0, 0, allow_small_or_imprecise_dtypes=True), [], ["iot"])
+    call("g", lambda e: e.iota(T["pidx"][:, :], [[1, 1]], 0, 1), [], ["pidx"])
+    call("g", lambda e: e.iota(T["p4"][:, :], [[1, 4]], 0, 4, allow_small_or_imprecise_dtypes=True), [], ["p4"])
+    send(["odi"], (ha, T["hod"][:, 0:9], T["odi"][:, 0:9], "hod", es[1::4]), (hc, T["hod"][:, 9:18], T["odi"][:, 9:18], "hod", es[3::4]))
+    arrived(["bi"], ("roda", back[0][0]), ("rodc", back[0][2]))
+    arrived(["bv"], ("riv", back[0][1]))
+    for t in range(3):
+        if t: arrived(["bw%d" % t], ("rw%d" % t, back[t][0]))
+        arrived(["rz%d" % t], ("rqa%d" % t, back[t][0]), ("rqb%d" % t, back[t][1]), ("rs%d" % t, back[t][2]))
+
+    ts(ci[:, :], iot[:, 0:C], -144.0, None, A.add, None, ["iot"], ["ci"])
+    ts(T["p15"][:, :], T["pidx"][:, :], 15, None, A.bitwise_and, None, ["pidx"], ["p15"])
+    vcopy(T["p16"][:, :], T["p15"][:, :], ["p15"], ["p16"])
+    ts(T["ofc"][:, :], iot[:, 0:36], 0.0, T["p16"][:, :], A.mult, A.add, ["iot", "p16"], ["ofc"])
+    ts(T["ne"][:, :], iot[:, 0:16], T["p16"][:, :], None, A.not_equal, None, ["iot", "p16"], ["ne"])
+    ts(T["nx"][:, :], iot[:, 0:16], T["p16"][:, :], 1.0, A.subtract, A.is_equal, ["iot", "p16"], ["nx"])
+    ts(T["t1"][:, :], T["nx"][:, :], 1048575.0, None, A.mult, None, ["nx"], ["t1"])
+    tt(T["sc16"][:, :], T["t1"][:, :], T["ne"][:, :], A.add, ["t1", "ne"], ["sc16"])
+    ts(T["sct"][:, :], T["p16"][:, :], 15.0, 1.0 - 2.0 ** -20, A.is_equal, A.mult, ["p16"], ["sct"])
+    ts(T["scol"][:, :], T["sct"][:, :], 2.0 ** -20, None, A.add, None, ["sct"], ["scol"])
+    scopy(T["scc"][:, :], T["sc16"][:, :].indirect(T["ofc"][:, :]), ["sc16", "ofc"], ["scc"])
+
+    def wrap(src, out, writes):
+        scan(T["zj"][:, :], T["scc"][:, 0:C], T[src][:, :], A.mult, A.add, ["scc", src], ["zj"])
+        ts(out, T["zj"][:, 15:C:16], T["scol"][:, :], 144.25, A.mult, A.add, ["zj", "scol"], writes)
+
+    vcopy(T["aw0"][:, 18:36], T["odi"][:, :], ["odi"], ["aw0.o"])
+    vcopy(T["ivr"][:, :].indirect(T["aw0"][:, 18:36]), ci[:, :], ["ci", "aw0.o"], ["ivr"])
+    wrap("ivr", T["aw0"][:, 0:18], ["aw0.i"])
+    send(["aw0.i"], (hb, T["hiv"][:, :], T["aw0"][:, 0:18], "hiv", es[0::2]))
+
+    def off(t, k):
+        return T["aw%d" % t][:, 0:18] if k == "i" else T["aw%d" % t][:, 18:36]
+
+    def keys(t):
+        tt(T["k0"][:, :], T["i5"][:, :].indirect(off(t, "i")), iot[:, 0:C], A.add, ["i5", "aw%d.i" % t, "iot"], ["k0"])
+        scopy(T["c0"][:, :], T["k0"][:, :], ["k0"], ["c0"])
+
+    def bank(p, b, n=C): return T[p][:, 512 * b:512 * b + n]
+
+    def part(name, b): return T[name][:, C * b:C * b + C]
+
+    def score(t):
+        q, s = T["xq%d" % t], T["xs%d" % t]
+        mm(bank("pr", 0), T["urq"][:, :], T["urp"][:, :], q[:, :], s[:, :], ["urq", "urp", "x%d" % t], ["pr0"])
+
+    def unpack(t, b):
+        q, s = T["xq%d" % t], T["xs%d" % t]
+        mm(bank("pd", b), T["eq"][:, 128 * b:128 * b + 128], T["ep"][:, 128 * b:128 * b + 128], q[:, :], s[:, :], ["e", "x%d" % t], ["pd%d" % b])
+
+    def held(b): scopy(part("fs", b), bank("pd", b), ["pd%d" % b], ["fs%d" % b])
+
+    def positive(): ts(T["fl"][:, :], bank("pr", 0), 0.0, None, A.is_gt, None, ["pr0"], ["fl"])
+
+    def chase(t, mid, late):
+        if t == 0:
+            vcopy(T["b0"][:, :], T["bi"][:, :], ["bi"], ["b0"])
+            scopy(T["jb"][:, :], ci[:, :].indirect(T["b0"][:, :]), ["ci", "b0"], ["jb"])
+            scopy(T["ja"][:, :], T["jb"][:, :].indirect(off(0, "i")), ["jb", "aw0.i"], ["ja"])
+        else:
+            scopy(T["ja"][:, :], T["op%d" % t][:, :].indirect(T["bw%d" % t][:, 0:18]), ["op%d" % t, "bw%d" % t], ["ja"])
+        wrap("ja", T["lo0"][:, :], ["lo0"])
+        jr, key, twin = "ja", "k0", "c0"
+        for i, r in enumerate(RAD):
+            last = i == len(RAD) - 1
+            lo = "lo%d" % i
+            if not last:
+                src = jr
+                for m in range(r - 1):
+                    dst = [x for x in ("ja", "jb", "jc") if x not in (src, jr)][0]
+                    scopy(T[dst][:, :], T[src][:, :].indirect(T[lo][:, :]), [src, lo], [dst])
+                    src = dst
+            acc = key
+            for m in range(r - 1):
+                if last and m == r - 2: name, out = "kk0", T["kk"][:, 0:C]
+                else:
+                    name = [x for x in ("k0", "k1", "k2") if x not in (acc, key)][0]
+                    out = T[name][:, :]
+                tt(out, T[acc][:, :].indirect(T[lo][:, :]), T[twin][:, :], A.min, [acc, twin, lo], [name])
+                acc = name
+            key = acc
+            if not last:
+                twin = "c1" if twin == "c0" else "c0"
+                scopy(T[twin][:, :], T[key][:, :], [key], [twin])
+            mid(i)
+            if not last:
+                jr = src
+                wrap(jr, T["lo%d" % (i + 1)][:, :], ["lo%d" % (i + 1)])
+            late(i)
+        scopy(T["kk"][:, C:2 * C], T["kk"][:, 0:C].indirect(off(t, "o")), ["kk0", "aw%d.o" % t], ["kk1"])
+        af = "af%d" % t
+        if t == 0:
+            vcopy(T["bf"][:, 0:18], T["bv"][:, :], ["bv"], ["bf.i"])
+            vcopy(T["bf"][:, 18:36], T["bi"][:, :], ["bi"], ["bf.o"])
+        else:
+            vcopy(T["bf"][:, :], T["bw%d" % t][:, :], ["bw%d" % t], ["bf.i", "bf.o"])
+        tt(T["df"][:, :], T["bf"][:, :], T[af][:, :], A.subtract, ["bf.i", "bf.o", af], ["df"])
+        scan(T["zk"][:, :], T["dkk"][:, :], T["kk"][:, :], A.add, A.max, ["dkk", "kk0", "kk1"], ["zk"])
+        vcopy(T["zki"][:, :], T["zk"][:, 15:2 * C:16], ["zk"], ["zki"])
+        ts(T["zkm"][:, :], T["zki"][:, :], 511, None, A.bitwise_and, None, ["zki"], ["zkm"])
+        vcopy(T["ll"][:, :], T["zkm"][:, :], ["zkm"], ["ll"])
+
+    def choose(t):
+        n = t + 1
+        af, bf, aw = "af%d" % t, "af%d" % n, "aw%d" % n
+        scopy(T["tf"][:, 0:C], T["fl"][:, :].indirect(T["ll"][:, 0:18]), ["fl", "ll"], ["tf0"])
+        vcopy(T["tf"][:, C:2 * C], T["fl"][:, :].indirect(T["ll"][:, 18:36]), ["fl", "ll"], ["tf1"])
+        scan(T["zf"][:, :], T["scc"][:, :], T["tf"][:, :], A.mult, A.add, ["scc", "tf0", "tf1"], ["zf"])
+        ts(T["fw"][:, :], T["zf"][:, 15:2 * C:16], T["scol"][:, :], 0.5, A.mult, A.is_ge, ["zf", "scol"], ["fw"])
+        tt(T["fm"][:, :], T["fw"][:, :], T["df"][:, :], A.mult, ["fw", "df"], ["fm"])
+        tt(T[bf][:, :], T["fm"][:, :], T[af][:, :], A.add, ["fm", af], [bf])
+        vcopy(T[aw][:, :], T[bf][:, :], [bf], [aw + ".i", aw + ".o"])
+        if n < 3:
+            send([aw + ".i"], (_helpers(core, dests[n], topo)[0], T["hw%d" % n][:, :], T[aw][:, :], "hw%d" % n, es[1::2]))
+
+    def means(t):
+        n = t + 1
+        o, ro = off(n, "o"), "aw%d.o" % n
+
+        def pair(b): tt(part("ys", b), part("gs", b), bank("pd", b), A.add, ["gs%d" % b, "pd%d" % b], ["ys%d" % b])
+        for b in range(3): scopy(part("gs", b), part("fs", b).indirect(o), ["fs%d" % b, ro], ["gs%d" % b])
+        vcopy(part("gs", 3), part("fs", 3).indirect(o), ["fs3", ro], ["gs3"])
+        for k, b in ("y0", "y3", "z0", "y1", "y2", "z1"):
+            b = int(b)
+            if k == "y": pair(b)
+            else: ts(T["zt"][:, b:4 * C:4], part("ys", b).indirect(o), 0.5, None, A.mult, None, ["ys%d" % b, ro], ["zt%d" % b])
+        for b in (3, 2): scopy(T["zt"][:, b:4 * C:4], part("ys", b).indirect(o), ["ys%d" % b, ro], ["zt%d" % b], 0.5)
+        zq, zs = T["zq%d" % t], T["zs%d" % t]
+        quant(zq[:, :], zs[:, :], T["zt"][:, :], ["zt0", "zt1", "zt2", "zt3"], ["z%d" % t])
+        a, b, c = _helpers(core, dests[t], topo)
+        hq, h = T["hq%d" % t], C // 2
+        send(["z%d" % t], (a, hq[:, 0:h].bitcast(dt.uint8), zq[:, 0:h].bitcast(dt.uint8), "hq%d" % t, es[1::2]),
+             (b, hq[:, h:C].bitcast(dt.uint8), zq[:, h:C].bitcast(dt.uint8), "hq%d" % t, es[0::2]))
+        send(["z%d" % t], (c, T["hs%d" % t][:, :], zs[:, :], "hs%d" % t, es))
+        if n < 3:
+            scopy(T["op%d" % n][:, :], ci[:, :].indirect(o), ["ci", ro], ["op%d" % n])
+            keys(n)
+        for b in (0, 2): scopy(part("fp", b), part("fs", b).indirect(o), ["fs%d" % b, ro], ["fp%d" % b], 32.0)
+
+    def layer(t):
+        n = t + 1
+        i, ri = off(n, "i"), "aw%d.i" % n
+        rq, rs = T["rq%d" % t], T["rs%d" % t]
+        for b in range(4):
+            mm(bank("pr", b), T["wq"][:, 128 * b:128 * b + 128], T["wp"][:, 128 * b:128 * b + 128], rq[:, :], rs[:, :], ["wq", "wp", "rz%d" % t], ["pr%d" % b])
+        for b in (0, 2): tt(part("rr", b), bank("pr", b), part("fp", b), A.add, ["pr%d" % b, "fp%d" % b], ["rr%d" % b])
+        for b in (1, 3):
+            scopy(part("rr", b), bank("pr", b), ["pr%d" % b], ["rr%d" % b], 0.03125)
+            scopy(T["xt"][:, b - 1:4 * C:4], part("rr", b - 1).indirect(i), ["rr%d" % (b - 1), ri], ["xt%d" % (b - 1)], 0.03125)
+            tt(T["xt"][:, b:4 * C:4], part("rr", b).indirect(i), part("fs", b), A.add, ["rr%d" % b, ri, "fs%d" % b], ["xt%d" % b])
+        quant(T["xq%d" % n][:, :], T["xs%d" % n][:, :], T["xt"][:, :], ["xt0", "xt1", "xt2", "xt3"], ["x%d" % n])
+        if n < 3:
+            score(n)
+            for b in range(4): unpack(n, b)
+
+    vcopy(T["af0"][:, :], T["aw0"][:, :], ["aw0.i", "aw0.o"], ["af0"])
+    ts(T["i5"][:, :], iot[:, 0:C], 512.0, None, A.mult, None, ["iot"], ["i5"])
+    keys(0)
+    ts(T["uof"][:, :], iot[:, 0:8], 16.0, None, A.mult, None, ["iot"], ["uof"])
+    quant(T["uq"][:, :], T["up"][:, :], T["uin"][:, :], ["uin"], ["u"])
+    vcopy(T["urq"][:, :].bitcast(dt.uint32), T["uq"][:, :].bitcast(dt.uint32).indirect(T["uof"][:, :]), ["u", "uof"], ["urq"])
+    vcopy(T["urp"][:, :], T["up"][:, :].indirect(T["uof"][:, :]), ["u", "uof"], ["urp"])
+    quant(T["xq0"][:, :], T["xs0"][:, :], T["xin"][:, :], ["xin"], ["x0"])
+    for b in range(4): ts(T["et"][:, 512 * b:512 * b + 512], iot[:, :], T["p4"][:, b:b + 1], None, A.is_equal, None, ["iot", "p4"], ["et%d" % b])
+    quant(T["eq"][:, :], T["ep"][:, :], T["et"][:, :], ["et0", "et1", "et2", "et3"], ["e"])
+    score(0)
+    for b in range(4): unpack(0, b)
+    for b in range(4): held(b)
+    positive()
+    ts(T["t1"][:, :], T["ne"][:, :], 1.0, 2.0 ** 20, A.subtract, A.mult, ["ne"], ["t1"])
+    ts(T["t2"][:, :], T["nx"][:, :], 2.0 ** 18, None, A.mult, None, ["nx"], ["t2"])
+    tt(T["dk16"][:, :], T["t1"][:, :], T["t2"][:, :], A.add, ["t1", "t2"], ["dk16"])
+    scopy(T["dkk"][:, :], T["dk16"][:, :].indirect(T["ofc"][:, :]), ["dk16", "ofc"], ["dkk"])
+    chase(0, lambda i: None, lambda i: None)
+    choose(0)
+    means(0)
+    for t in (1, 2):
+        def mid(i):
+            if i == MID: layer(t - 1)
+
+        def late(i):
+            if i == MID: positive()
+            last = len(RAD) - 1
+            for b in range(4):
+                if i == min(MID + b, last): held(b)
+        chase(t, mid, late)
+        choose(t)
+        means(t)
+    quant(T["vq"][:, :], T["vp"][:, :], T["vin"][:, :], ["vin"], ["v"])
+    vcopy(T["fr"][:, :], iot[:, 0:C].indirect(off(3, "o")), ["iot", "aw3.o"], ["fr"])
+    for k in range(8): store("y", T.fo[k:k + 1, :], T["fr"][16 * k:16 * k + 1, :], ["fr"])
+    layer(2)
+    store("y", T.oc[:, :], T["xq3"][:, :].bitcast(dt.uint8), ["x3"])
+    mm(bank("pr", 0), T["vq"][:, :], T["vp"][:, :], T["xq3"][:, :], T["xs3"][:, :], ["v", "x3"], ["pr0"])
+    vcopy(T["yo"][:, :], bank("pr", 0), ["pr0"], ["yo"])
+    for k in range(4): store("s", T.osc[4 * k:4 * k + 4, :], T["xs3"][32 * k:32 * k + 4, :], ["x3"])
+    store("y", T.y[:, :], T["yo"][:, :], ["yo"])
+    for s in ("cv", "cs", "ct", "cg", "store"): g.wait_ge(T.sem[s], count[s])
+    g.wait_ge(T.sem["sent"], sent[0])

@@ -4,7 +4,7 @@ from concourse.mybir import dt, AluOpType, ActivationFunctionType
 C = 288
 STEP = [4, 1, 2]
 RAD = [2, 2, 2, 2, 2, 3, 3]
-MID = 4
+SUMMED = (0, 2)
 F32, BF, I32, U16, U8, MX = "float32", "bfloat16", "int32", "uint16", "uint8", "float8_e4m3fn_x4"
 
 
@@ -13,16 +13,16 @@ def _scratch():
 
     def sb(dtype, **names):
         for k in names: s[k] = ("sbuf", [128, names[k]], dtype)
-    sb(I32, odi=18, bi=18, hod=18, pidx=1, p15=1, zki=36, zkm=36)
-    sb(U16, ofc=36, uof=8, b0=18, bv=18, hiv=18, ll=36)
+    sb(I32, odi=18, bi=18, hod=18, ivi=18, bv=18, hiv=18, pidx=1, p15=1, zki=36, zkm=36)
+    sb(U16, ofc=36, uof=8, b0=18, ll=36)
     for k in range(4): sb(U16, **{"aw%d" % k: 36})
-    for k in (1, 2): sb(U16, **{"hw%d" % k: 36, "bw%d" % k: 36})
+    for k in (1, 2): sb(U16, **{a + "%d" % k: 18 for a in ("hw", "bw", "hx", "bx")})
     for k in range(len(RAD)): sb(U16, **{"lo%d" % k: 18})
     sb(BF, xin=4 * C, uin=512, vin=512, et=2048, zt=4 * C, xt=4 * C)
     sb(BF, ci=C, scc=2 * C, ivr=C, ja=C, jb=C, jc=C, zj=C, fl=C, tf=2 * C, zf=2 * C)
     for k in (1, 2): sb(BF, **{"op%d" % k: C})
     sb(F32, iot=512, i5=C, p4=4, p16=1, sct=1, scol=1, ne=16, nx=16, t1=16, t2=16, sc16=16, dk16=16, dkk=2 * C)
-    sb(F32, k0=C, k1=C, k2=C, c0=C, c1=C, gs=4 * C, kk=2 * C, zk=2 * C, bf=36, df=36, fw=36, fm=36, af0=36, af1=36, af2=36, af3=36)
+    sb(F32, k0=C, k1=C, k2=C, c0=C, c1=C, gs=4 * C, kk=2 * C, zk=2 * C, bf=36, df=36, ds=36, fw=36, fm=36, af0=36, af1=36, af2=36, af3=36)
     sb(F32, fs=4 * C, ys=4 * C, fp=4 * C, rr=4 * C, yo=C, fr=C)
     for k, n in (("w", 512), ("e", 512), ("u", 128), ("ur", 128), ("v", 128)): sb(MX, **{k + "q": n}); sb(U8, **{k + "p": n})
     for k in range(4): sb(MX, **{"xq%d" % k: C}); sb(U8, **{"xs%d" % k: C})
@@ -35,8 +35,8 @@ def _scratch():
 
 SCRATCH = _scratch()
 SEMAPHORES = ["cv", "cs", "ct", "cg", "lod", "lx", "lu", "lv", "lwc", "lws", "store", "sent",
-              "hod", "hiv", "hw1", "hw2", "hq0", "hq1", "hq2", "hs0", "hs1", "hs2",
-              "roda", "rodc", "riv", "rw1", "rw2", "rqa0", "rqa1", "rqa2", "rqb0", "rqb1", "rqb2", "rs0", "rs1", "rs2"]
+              "hod", "hiv", "hw1", "hw2", "hx1", "hx2", "rx1", "rx2", "hq0", "hq1", "hq2", "hs0", "hs1", "hs2",
+              "roda", "rivb", "rivc", "rw1", "rw2", "rqa0", "rqa1", "rqa2", "rqb0", "rqb1", "rqb2", "rs0", "rs1", "rs2"]
 
 
 def _mask(es):
@@ -64,16 +64,16 @@ def _relay(g, core, rc, T, topo):
     for t, dest in enumerate(dests):
         a, b, c = _helpers(rc, dest, topo)
         if t == 0:
-            for h, lo, sem in ((a, 0, "roda"), (c, 9, "rodc")):
+            if core == a:
+                g.wait_ge(T.sem["hod"], on_chip(2))
+                n += fwd(dest, T["bi"][:, :], T["hod"][:, :], "roda")
+            for h, lo, sem in ((b, 0, "rivb"), (c, 9, "rivc")):
                 if core == h:
-                    g.wait_ge(T.sem["hod"], on_chip(4))
-                    n += fwd(dest, T["bi"][:, lo:lo + 9], T["hod"][:, lo:lo + 9], sem)
-            if core == b:
-                g.wait_ge(T.sem["hiv"], on_chip(2))
-                n += fwd(dest, T["bv"][:, :], T["hiv"][:, :], "riv")
+                    g.wait_ge(T.sem["hiv"], on_chip(4))
+                    n += fwd(dest, T["bv"][:, lo:lo + 9], T["hiv"][:, lo:lo + 9], sem)
         if t < 2 and core == _helpers(rc, dests[t + 1], topo)[0]:
             k = "w%d" % (t + 1)
-            g.wait_ge(T.sem["h" + k], on_chip(2))
+            g.wait_ge(T.sem["h" + k], on_chip(1))
             n += fwd(dests[t + 1], T["b" + k][:, :], T["h" + k][:, :], "r" + k)
         for h, lo, sem in ((a, 0, "rqa"), (b, C // 2, "rqb")):
             if core == h:
@@ -84,6 +84,10 @@ def _relay(g, core, rc, T, topo):
             k = "s%d" % t
             g.wait_ge(T.sem["h" + k], on_chip(1))
             n += fwd(dest, T["r" + k][:, :], T["h" + k][:, :], "r" + k)
+        if t < 2 and core == _helpers(rc, dests[t + 1], topo)[2]:
+            k = "x%d" % (t + 1)
+            g.wait_ge(T.sem["h" + k], on_chip(1))
+            n += fwd(dests[t + 1], T["b" + k][:, :], T["h" + k][:, :], "r" + k)
     if n: g.wait_ge(T.sem["sent"], n)
 
 
@@ -94,7 +98,7 @@ def rank_program(g, core, T, topo):
             if T.rank_of(c) is not None: _relay(g, core, c, T, topo)
         return
     A = AluOpType
-    COPY = ActivationFunctionType.Copy
+    COPY, RELU, SIGN = ActivationFunctionType.Copy, ActivationFunctionType.Relu, ActivationFunctionType.Sign
     eng = {"v": g.vector, "s": g.scalar, "t": g.tensor, "y": g.sync, "g": g}
     count, last_write, readers = {}, {}, {}
     known = {q: {} for q in eng}
@@ -179,11 +183,13 @@ def rank_program(g, core, T, topo):
     call("g", lambda e: e.iota(iot[:, :], [[1, 512]], 0, 0, allow_small_or_imprecise_dtypes=True), [], ["iot"])
     call("g", lambda e: e.iota(T["pidx"][:, :], [[1, 1]], 0, 1), [], ["pidx"])
     call("g", lambda e: e.iota(T["p4"][:, :], [[1, 4]], 0, 4, allow_small_or_imprecise_dtypes=True), [], ["p4"])
-    send(["odi"], (ha, T["hod"][:, 0:9], T["odi"][:, 0:9], "hod", es[1::4]), (hc, T["hod"][:, 9:18], T["odi"][:, 9:18], "hod", es[3::4]))
-    arrived(["bi"], ("roda", back[0][0]), ("rodc", back[0][2]))
-    arrived(["bv"], ("riv", back[0][1]))
+    send(["odi"], (ha, T["hod"][:, :], T["odi"][:, :], "hod", es[1::2]))
+    arrived(["bi"], ("roda", back[0][0]))
+    arrived(["bv"], ("rivb", back[0][1]), ("rivc", back[0][2]))
     for t in range(3):
-        if t: arrived(["bw%d" % t], ("rw%d" % t, back[t][0]))
+        if t:
+            arrived(["bw%d" % t], ("rw%d" % t, back[t][0]))
+            arrived(["bx%d" % t], ("rx%d" % t, back[t][2]))
         arrived(["rz%d" % t], ("rqa%d" % t, back[t][0]), ("rqb%d" % t, back[t][1]), ("rs%d" % t, back[t][2]))
 
     ts(ci[:, :], iot[:, 0:C], -144.0, None, A.add, None, ["iot"], ["ci"])
@@ -205,14 +211,14 @@ def rank_program(g, core, T, topo):
     vcopy(T["aw0"][:, 18:36], T["odi"][:, :], ["odi"], ["aw0.o"])
     vcopy(T["ivr"][:, :].indirect(T["aw0"][:, 18:36]), ci[:, :], ["ci", "aw0.o"], ["ivr"])
     wrap("ivr", T["aw0"][:, 0:18], ["aw0.i"])
-    send(["aw0.i"], (hb, T["hiv"][:, :], T["aw0"][:, 0:18], "hiv", es[0::2]))
+    vcopy(T["ivi"][:, :], T["aw0"][:, 0:18], ["aw0.i"], ["ivi"])
+    send(["ivi"], (hb, T["hiv"][:, 0:9], T["ivi"][:, 0:9], "hiv", es[0::4]), (hc, T["hiv"][:, 9:18], T["ivi"][:, 9:18], "hiv", es[2::4]))
 
     def off(t, k):
         return T["aw%d" % t][:, 0:18] if k == "i" else T["aw%d" % t][:, 18:36]
 
     def keys(t):
         tt(T["k0"][:, :], T["i5"][:, :].indirect(off(t, "i")), iot[:, 0:C], A.add, ["i5", "aw%d.i" % t, "iot"], ["k0"])
-        scopy(T["c0"][:, :], T["k0"][:, :], ["k0"], ["c0"])
 
     def bank(p, b, n=C): return T[p][:, 512 * b:512 * b + n]
 
@@ -228,15 +234,18 @@ def rank_program(g, core, T, topo):
 
     def held(b): scopy(part("fs", b), bank("pd", b), ["pd%d" % b], ["fs%d" % b])
 
-    def positive(): ts(T["fl"][:, :], bank("pr", 0), 0.0, None, A.is_gt, None, ["pr0"], ["fl"])
+    def signs(): call("s", lambda e: e.activation(T["fl"][:, :], bank("pr", 0), SIGN), ["pr0"], ["fl"])
 
-    def chase(t, mid, late):
+    def shifted(out, in_, reads, writes): ts(out, in_, 0.25, None, A.add, None, reads, writes)
+
+    def chase(t, mid):
         if t == 0:
             vcopy(T["b0"][:, :], T["bi"][:, :], ["bi"], ["b0"])
             scopy(T["jb"][:, :], ci[:, :].indirect(T["b0"][:, :]), ["ci", "b0"], ["jb"])
             scopy(T["ja"][:, :], T["jb"][:, :].indirect(off(0, "i")), ["jb", "aw0.i"], ["ja"])
         else:
             scopy(T["ja"][:, :], T["op%d" % t][:, :].indirect(T["bw%d" % t][:, 0:18]), ["op%d" % t, "bw%d" % t], ["ja"])
+        scopy(T["c0"][:, :], T["k0"][:, :], ["k0"], ["c0"])
         wrap("ja", T["lo0"][:, :], ["lo0"])
         jr, key, twin = "ja", "k0", "c0"
         for i, r in enumerate(RAD):
@@ -256,53 +265,77 @@ def rank_program(g, core, T, topo):
                     out = T[name][:, :]
                 tt(out, T[acc][:, :].indirect(T[lo][:, :]), T[twin][:, :], A.min, [acc, twin, lo], [name])
                 acc = name
+                if last and m == 0: mid()
             key = acc
             if not last:
                 twin = "c1" if twin == "c0" else "c0"
                 scopy(T[twin][:, :], T[key][:, :], [key], [twin])
-            mid(i)
-            if not last:
                 jr = src
                 wrap(jr, T["lo%d" % (i + 1)][:, :], ["lo%d" % (i + 1)])
-            late(i)
-        scopy(T["kk"][:, C:2 * C], T["kk"][:, 0:C].indirect(off(t, "o")), ["kk0", "aw%d.o" % t], ["kk1"])
-        af = "af%d" % t
-        if t == 0:
-            vcopy(T["bf"][:, 0:18], T["bv"][:, :], ["bv"], ["bf.i"])
-            vcopy(T["bf"][:, 18:36], T["bi"][:, :], ["bi"], ["bf.o"])
-        else:
-            vcopy(T["bf"][:, :], T["bw%d" % t][:, :], ["bw%d" % t], ["bf.i", "bf.o"])
-        tt(T["df"][:, :], T["bf"][:, :], T[af][:, :], A.subtract, ["bf.i", "bf.o", af], ["df"])
-        scan(T["zk"][:, :], T["dkk"][:, :], T["kk"][:, :], A.add, A.max, ["dkk", "kk0", "kk1"], ["zk"])
-        vcopy(T["zki"][:, :], T["zk"][:, 15:2 * C:16], ["zk"], ["zki"])
-        ts(T["zkm"][:, :], T["zki"][:, :], 511, None, A.bitwise_and, None, ["zki"], ["zkm"])
-        vcopy(T["ll"][:, :], T["zkm"][:, :], ["zkm"], ["ll"])
+
+    def spread(h):
+        k, a, b = str(h), C * h, C * h + C
+        scan(T["zk"][:, a:b], T["dkk"][:, a:b], T["kk"][:, a:b], A.add, A.max, ["dkk", "kk" + k], ["zk" + k])
 
     def choose(t):
         n = t + 1
-        af, bf, aw = "af%d" % t, "af%d" % n, "aw%d" % n
-        scopy(T["tf"][:, 0:C], T["fl"][:, :].indirect(T["ll"][:, 0:18]), ["fl", "ll"], ["tf0"])
-        vcopy(T["tf"][:, C:2 * C], T["fl"][:, :].indirect(T["ll"][:, 18:36]), ["fl", "ll"], ["tf1"])
-        scan(T["zf"][:, :], T["scc"][:, :], T["tf"][:, :], A.mult, A.add, ["scc", "tf0", "tf1"], ["zf"])
-        ts(T["fw"][:, :], T["zf"][:, 15:2 * C:16], T["scol"][:, :], 0.5, A.mult, A.is_ge, ["zf", "scol"], ["fw"])
-        tt(T["fm"][:, :], T["fw"][:, :], T["df"][:, :], A.mult, ["fw", "df"], ["fm"])
-        tt(T[bf][:, :], T["fm"][:, :], T[af][:, :], A.add, ["fm", af], [bf])
-        vcopy(T[aw][:, :], T[bf][:, :], [bf], [aw + ".i", aw + ".o"])
-        if n < 3:
-            send([aw + ".i"], (_helpers(core, dests[n], topo)[0], T["hw%d" % n][:, :], T[aw][:, :], "hw%d" % n, es[1::2]))
+        af, aw = "af%d" % t, "aw%d" % n
+
+        def leaders(h):
+            k = str(h)
+            a, b = 18 * h, 18 * h + 18
+            vcopy(T["zki"][:, a:b], T["zk"][:, C * h + 15:C * h + C:16], ["zk" + k], ["zki" + k])
+            ts(T["zkm"][:, a:b], T["zki"][:, a:b], 511, None, A.bitwise_and, None, ["zki" + k], ["zkm" + k])
+            vcopy(T["ll"][:, a:b], T["zkm"][:, a:b], ["zkm" + k], ["ll" + k])
+
+        def flags(h):
+            k = str(h)
+            call("s", lambda e: e.activation(T["tf"][:, C * h:C * h + C], T["fl"][:, :].indirect(T["ll"][:, 18 * h:18 * h + 18]), RELU), ["fl", "ll" + k], ["tf" + k])
+
+        def take(h):
+            k, r = str(h), aw + (".i", ".o")[h]
+            a, b = C * h, C * h + C
+            scan(T["zf"][:, a:b], T["scc"][:, a:b], T["tf"][:, a:b], A.mult, A.add, ["scc", "tf" + k], ["zf" + k])
+            a, b = 18 * h, 18 * h + 18
+            tt(T["fm"][:, a:b], T["zf"][:, C * h + 15:C * h + C:16], T["ds"][:, a:b], A.mult, ["zf" + k, "ds"], ["fm" + k])
+            tt(T["fw"][:, a:b], T["fm"][:, a:b], T[af][:, a:b], A.add, ["fm" + k, af], ["fw" + k])
+            vcopy(T[aw][:, a:b], T["fw"][:, a:b], ["fw" + k], [r])
+        scopy(T["kk"][:, C:2 * C], T["kk"][:, 0:C].indirect(off(t, "o")), ["kk0", "aw%d.o" % t], ["kk1"])
+        leaders(0)
+        signs()
+        if t == 0:
+            shifted(T["bf"][:, 0:18], T["bv"][:, :], ["bv"], ["bf.i"])
+            shifted(T["bf"][:, 18:36], T["bi"][:, :], ["bi"], ["bf.o"])
+        else:
+            shifted(T["bf"][:, 0:18], T["bw%d" % t][:, :], ["bw%d" % t], ["bf.i"])
+            shifted(T["bf"][:, 18:36], T["bx%d" % t][:, :], ["bx%d" % t], ["bf.o"])
+        tt(T["df"][:, :], T["bf"][:, :], T[af][:, :], A.subtract, ["bf.i", "bf.o", af], ["df"])
+        ts(T["ds"][:, :], T["df"][:, :], T["scol"][:, :], None, A.mult, None, ["df", "scol"], ["ds"])
+        flags(0)
+        spread(1)
+        leaders(1)
+        if t: held(0)
+        flags(1)
+        take(0)
+        if n < 3: send([aw + ".i"], (_helpers(core, dests[n], topo)[0], T["hw%d" % n][:, :], T[aw][:, 0:18], "hw%d" % n, es))
+        take(1)
+        if t:
+            for b in (1, 2): held(b)
 
     def means(t):
         n = t + 1
         o, ro = off(n, "o"), "aw%d.o" % n
 
         def pair(b): tt(part("ys", b), part("gs", b), bank("pd", b), A.add, ["gs%d" % b, "pd%d" % b], ["ys%d" % b])
-        for b in range(3): scopy(part("gs", b), part("fs", b).indirect(o), ["fs%d" % b, ro], ["gs%d" % b])
-        vcopy(part("gs", 3), part("fs", 3).indirect(o), ["fs3", ro], ["gs3"])
-        for k, b in ("y0", "y3", "z0", "y1", "y2", "z1"):
+        for b in (1, 2, 3):
+            scopy(part("gs", b), part("fs", b).indirect(o), ["fs%d" % b, ro], ["gs%d" % b])
+            if t and b == 1: held(3)
+        vcopy(part("gs", 0), part("fs", 0).indirect(o), ["fs0", ro], ["gs0"])
+        for k, b in ("y1", "y0", "z1", "y2", "y3", "z2"):
             b = int(b)
             if k == "y": pair(b)
             else: ts(T["zt"][:, b:4 * C:4], part("ys", b).indirect(o), 0.5, None, A.mult, None, ["ys%d" % b, ro], ["zt%d" % b])
-        for b in (3, 2): scopy(T["zt"][:, b:4 * C:4], part("ys", b).indirect(o), ["ys%d" % b, ro], ["zt%d" % b], 0.5)
+        for b in (0, 3): scopy(T["zt"][:, b:4 * C:4], part("ys", b).indirect(o), ["ys%d" % b, ro], ["zt%d" % b], 0.5)
         zq, zs = T["zq%d" % t], T["zs%d" % t]
         quant(zq[:, :], zs[:, :], T["zt"][:, :], ["zt0", "zt1", "zt2", "zt3"], ["z%d" % t])
         a, b, c = _helpers(core, dests[t], topo)
@@ -311,67 +344,74 @@ def rank_program(g, core, T, topo):
              (b, hq[:, h:C].bitcast(dt.uint8), zq[:, h:C].bitcast(dt.uint8), "hq%d" % t, es[0::2]))
         send(["z%d" % t], (c, T["hs%d" % t][:, :], zs[:, :], "hs%d" % t, es))
         if n < 3:
+            send([ro], (_helpers(core, dests[n], topo)[2], T["hx%d" % n][:, :], o, "hx%d" % n, es))
             scopy(T["op%d" % n][:, :], ci[:, :].indirect(o), ["ci", ro], ["op%d" % n])
             keys(n)
-        for b in (0, 2): scopy(part("fp", b), part("fs", b).indirect(o), ["fs%d" % b, ro], ["fp%d" % b], 32.0)
+            shifted(T["af%d" % n][:, :], T["aw%d" % n][:, :], ["aw%d.i" % n, "aw%d.o" % n], ["af%d" % n])
+        for b in SUMMED: scopy(part("fp", b), part("fs", b).indirect(o), ["fs%d" % b, ro], ["fp%d" % b], 32.0)
 
-    def layer(t):
+    def products(t):
         n = t + 1
         i, ri = off(n, "i"), "aw%d.i" % n
         rq, rs = T["rq%d" % t], T["rs%d" % t]
         for b in range(4):
             mm(bank("pr", b), T["wq"][:, 128 * b:128 * b + 128], T["wp"][:, 128 * b:128 * b + 128], rq[:, :], rs[:, :], ["wq", "wp", "rz%d" % t], ["pr%d" % b])
-        for b in (0, 2): tt(part("rr", b), bank("pr", b), part("fp", b), A.add, ["pr%d" % b, "fp%d" % b], ["rr%d" % b])
-        for b in (1, 3):
-            scopy(part("rr", b), bank("pr", b), ["pr%d" % b], ["rr%d" % b], 0.03125)
-            scopy(T["xt"][:, b - 1:4 * C:4], part("rr", b - 1).indirect(i), ["rr%d" % (b - 1), ri], ["xt%d" % (b - 1)], 0.03125)
-            tt(T["xt"][:, b:4 * C:4], part("rr", b).indirect(i), part("fs", b), A.add, ["rr%d" % b, ri, "fs%d" % b], ["xt%d" % b])
+        for b in SUMMED: tt(part("rr", b), bank("pr", b), part("fp", b), A.add, ["pr%d" % b, "fp%d" % b], ["rr%d" % b])
+
+        def scaled(b): scopy(part("rr", b), bank("pr", b), ["pr%d" % b], ["rr%d" % b], 0.03125)
+
+        def moved(b): scopy(T["xt"][:, b:4 * C:4], part("rr", b).indirect(i), ["rr%d" % b, ri], ["xt%d" % b], 0.03125)
+        for f, b in ((scaled, 1), (moved, 0), (scaled, 3), (moved, 2)): f(b)
+
+    def state(t):
+        n = t + 1
+        i, ri = off(n, "i"), "aw%d.i" % n
+        for b in range(4):
+            if b not in SUMMED: tt(T["xt"][:, b:4 * C:4], part("rr", b).indirect(i), part("fs", b), A.add, ["rr%d" % b, ri, "fs%d" % b], ["xt%d" % b])
+        if n < 3: spread(0)
         quant(T["xq%d" % n][:, :], T["xs%d" % n][:, :], T["xt"][:, :], ["xt0", "xt1", "xt2", "xt3"], ["x%d" % n])
         if n < 3:
             score(n)
             for b in range(4): unpack(n, b)
 
-    vcopy(T["af0"][:, :], T["aw0"][:, :], ["aw0.i", "aw0.o"], ["af0"])
-    ts(T["i5"][:, :], iot[:, 0:C], 512.0, None, A.mult, None, ["iot"], ["i5"])
-    keys(0)
-    ts(T["uof"][:, :], iot[:, 0:8], 16.0, None, A.mult, None, ["iot"], ["uof"])
-    quant(T["uq"][:, :], T["up"][:, :], T["uin"][:, :], ["uin"], ["u"])
-    vcopy(T["urq"][:, :].bitcast(dt.uint32), T["uq"][:, :].bitcast(dt.uint32).indirect(T["uof"][:, :]), ["u", "uof"], ["urq"])
-    vcopy(T["urp"][:, :], T["up"][:, :].indirect(T["uof"][:, :]), ["u", "uof"], ["urp"])
-    quant(T["xq0"][:, :], T["xs0"][:, :], T["xin"][:, :], ["xin"], ["x0"])
-    for b in range(4): ts(T["et"][:, 512 * b:512 * b + 512], iot[:, :], T["p4"][:, b:b + 1], None, A.is_equal, None, ["iot", "p4"], ["et%d" % b])
-    quant(T["eq"][:, :], T["ep"][:, :], T["et"][:, :], ["et0", "et1", "et2", "et3"], ["e"])
-    score(0)
-    for b in range(4): unpack(0, b)
-    for b in range(4): held(b)
-    positive()
     ts(T["t1"][:, :], T["ne"][:, :], 1.0, 2.0 ** 20, A.subtract, A.mult, ["ne"], ["t1"])
     ts(T["t2"][:, :], T["nx"][:, :], 2.0 ** 18, None, A.mult, None, ["nx"], ["t2"])
     tt(T["dk16"][:, :], T["t1"][:, :], T["t2"][:, :], A.add, ["t1", "t2"], ["dk16"])
     scopy(T["dkk"][:, :], T["dk16"][:, :].indirect(T["ofc"][:, :]), ["dk16", "ofc"], ["dkk"])
-    chase(0, lambda i: None, lambda i: None)
+    ts(T["i5"][:, :], iot[:, 0:C], 512.0, None, A.mult, None, ["iot"], ["i5"])
+    keys(0)
+    ts(T["uof"][:, :], iot[:, 0:8], 16.0, None, A.mult, None, ["iot"], ["uof"])
+    for b in range(4): ts(T["et"][:, 512 * b:512 * b + 512], iot[:, :], T["p4"][:, b:b + 1], None, A.is_equal, None, ["iot", "p4"], ["et%d" % b])
+    quant(T["eq"][:, :], T["ep"][:, :], T["et"][:, :], ["et0", "et1", "et2", "et3"], ["e"])
+    quant(T["xq0"][:, :], T["xs0"][:, :], T["xin"][:, :], ["xin"], ["x0"])
+    for b in range(4): unpack(0, b)
+    for b in range(4): held(b)
+    quant(T["uq"][:, :], T["up"][:, :], T["uin"][:, :], ["uin"], ["u"])
+    vcopy(T["urq"][:, :].bitcast(dt.uint32), T["uq"][:, :].bitcast(dt.uint32).indirect(T["uof"][:, :]), ["u", "uof"], ["urq"])
+    vcopy(T["urp"][:, :], T["up"][:, :].indirect(T["uof"][:, :]), ["u", "uof"], ["urp"])
+    score(0)
+    shifted(T["af0"][:, :], T["aw0"][:, :], ["aw0.i", "aw0.o"], ["af0"])
+    chase(0, lambda: None)
+    spread(0)
     choose(0)
     means(0)
     for t in (1, 2):
-        def mid(i):
-            if i == MID: layer(t - 1)
-
-        def late(i):
-            if i == MID: positive()
-            last = len(RAD) - 1
-            for b in range(4):
-                if i == min(MID + b, last): held(b)
-        chase(t, mid, late)
+        chase(t, lambda: products(t - 1))
+        state(t - 1)
         choose(t)
         means(t)
     quant(T["vq"][:, :], T["vp"][:, :], T["vin"][:, :], ["vin"], ["v"])
     vcopy(T["fr"][:, :], iot[:, 0:C].indirect(off(3, "o")), ["iot", "aw3.o"], ["fr"])
     for k in range(8): store("y", T.fo[k:k + 1, :], T["fr"][16 * k:16 * k + 1, :], ["fr"])
-    layer(2)
+    products(2)
+    state(2)
     store("y", T.oc[:, :], T["xq3"][:, :].bitcast(dt.uint8), ["x3"])
-    mm(bank("pr", 0), T["vq"][:, :], T["vp"][:, :], T["xq3"][:, :], T["xs3"][:, :], ["v", "x3"], ["pr0"])
-    vcopy(T["yo"][:, :], bank("pr", 0), ["pr0"], ["yo"])
-    for k in range(4): store("s", T.osc[4 * k:4 * k + 4, :], T["xs3"][32 * k:32 * k + 4, :], ["x3"])
-    store("y", T.y[:, :], T["yo"][:, :], ["yo"])
+    h = C // 2
+    for k in range(2): mm(bank("pr", k, h), T["vq"][:, :], T["vp"][:, :], T["xq3"][:, h * k:h * k + h], T["xs3"][:, h * k:h * k + h], ["v", "x3"], ["pr%d" % k])
+    for k in range(4): store("y" if k < 2 else "s", T.osc[4 * k:4 * k + 4, :], T["xs3"][32 * k:32 * k + 4, :], ["x3"])
+    vcopy(T["yo"][:, 0:h], bank("pr", 0, h), ["pr0"], ["yo0"])
+    scopy(T["yo"][:, h:C], bank("pr", 1, h), ["pr1"], ["yo1"])
+    store("y", T.y[:, 0:h], T["yo"][:, 0:h], ["yo0"])
+    store("s", T.y[:, h:C], T["yo"][:, h:C], ["yo1"])
     for s in ("cv", "cs", "ct", "cg", "store"): g.wait_ge(T.sem[s], count[s])
     g.wait_ge(T.sem["sent"], sent[0])

from concourse.bass import DstId, RemoteDMATransfer
from concourse.mybir import dt, AluOpType, ActivationFunctionType

C = 288
STEP = [4, 1, 2]
RAD = [2, 2, 2, 2, 2, 3, 3]
SUMMED = (0, 2)
F32, BF, I32, U16, U8, MX = "float32", "bfloat16", "int32", "uint16", "uint8", "float8_e4m3fn_x4"


def _scratch():
    s = {}

    def sb(dtype, **names):
        for k in names: s[k] = ("sbuf", [128, names[k]], dtype)
    sb(I32, odi=18, bi=18, hod=18, ivi=18, bv=18, hiv=18, pidx=1, p15=1, zki=36, zkm=36)
    sb(U16, ofc=36, uof=8, b0=18, ll=36)
    for k in range(4): sb(U16, **{"aw%d" % k: 36})
    for k in (1, 2): sb(U16, **{a + "%d" % k: 18 for a in ("hw", "bw", "hx", "bx")})
    for k in range(len(RAD)): sb(U16, **{"lo%d" % k: 18})
    sb(BF, xin=4 * C, uin=512, vin=512, et=2048, zt=4 * C, xt=4 * C)
    sb(BF, ci=C, scc=2 * C, ivr=C, ja=C, jb=C, jc=C, zj=C, fl=C, tf=2 * C, zf=2 * C)
    for k in (1, 2): sb(BF, **{"op%d" % k: C})
    sb(F32, iot=512, i5=C, p4=4, p16=1, sct=1, scol=1, ne=16, nx=16, t1=16, t2=16, sc16=16, dk16=16, dkk=2 * C)
    sb(F32, k0=C, k1=C, k2=C, c0=C, c1=C, gs=4 * C, kk=2 * C, zk=2 * C, bf=36, df=36, ds=36, fw=36, fm=36, af0=36, af1=36, af2=36, af3=36)
    sb(F32, fs=4 * C, ys=4 * C, fp=4 * C, rr=4 * C, yo=C, fr=C)
    for k, n in (("w", 512), ("e", 512), ("u", 128), ("ur", 128), ("v", 128)): sb(MX, **{k + "q": n}); sb(U8, **{k + "p": n})
    for k in range(4): sb(MX, **{"xq%d" % k: C}); sb(U8, **{"xs%d" % k: C})
    for k in range(3):
        for a in "zhr": sb(MX, **{"%sq%d" % (a, k): C}); sb(U8, **{"%ss%d" % (a, k): C})
    s["pd"] = ("psum", [128, 2048], F32)
    s["pr"] = ("psum", [128, 2048], F32)
    return s


SCRATCH = _scratch()
SEMAPHORES = ["cv", "cs", "ct", "cg", "lod", "lx", "lu", "lv", "lwc", "lws", "store", "sent",
              "hod", "hiv", "hw1", "hw2", "hx1", "hx2", "rx1", "rx2", "hq0", "hq1", "hq2", "hs0", "hs1", "hs2",
              "roda", "rivb", "rivc", "rw1", "rw2", "rqa0", "rqa1", "rqa2", "rqb0", "rqb1", "rqb2", "rs0", "rs1", "rs2"]


def _mask(es):
    return sum(1 << e for e in es)


def _helpers(rc, dest, topo):
    h = [c for c in topo.cores_of(rc) if c != rc and topo.may_write(c, dest)]
    near = [c for c in h if topo.die(c) == topo.die(rc)]
    far = [c for c in h if topo.die(c) != topo.die(rc)]
    return near[0], far[0], near[1]


def _relay(g, core, rc, T, topo):
    rank, n = T.rank_of(rc), 0

    def fwd(dest, dst, src, sem):
        rid, pid = topo.addr(dest, core)
        g.remote_dma(out_ap=dst, in_ap=src, remote_sem=T.sem[sem], local_sem=T.sem["sent"], pid=pid, routing_id=rid, dma_engine_mask=topo.mask(core, dest))
        return len(topo.engines(core, dest))

    def on_chip(k):
        return len(topo.engines(rc, core)) // k
    dests = [T.cores[rank ^ s] for s in STEP]
    for t, dest in enumerate(dests):
        a, b, c = _helpers(rc, dest, topo)
        if t == 0:
            if core == a:
                g.wait_ge(T.sem["hod"], on_chip(2))
                n += fwd(dest, T["bi"][:, :], T["hod"][:, :], "roda")
            for h, lo, sem in ((b, 0, "rivb"), (c, 9, "rivc")):
                if core == h:
                    g.wait_ge(T.sem["hiv"], on_chip(4))
                    n += fwd(dest, T["bv"][:, lo:lo + 9], T["hiv"][:, lo:lo + 9], sem)
        if t < 2 and core == _helpers(rc, dests[t + 1], topo)[0]:
            k = "w%d" % (t + 1)
            g.wait_ge(T.sem["h" + k], on_chip(1))
            n += fwd(dests[t + 1], T["b" + k][:, :], T["h" + k][:, :], "r" + k)
        for h, lo, sem in ((a, 0, "rqa"), (b, C // 2, "rqb")):
            if core == h:
                k = "q%d" % t
                g.wait_ge(T.sem["h" + k], on_chip(2))
                n += fwd(dest, T["r" + k][:, lo:lo + C // 2].bitcast(dt.uint8), T["h" + k][:, lo:lo + C // 2].bitcast(dt.uint8), "%s%d" % (sem, t))
        if core == c:
            k = "s%d" % t
            g.wait_ge(T.sem["h" + k], on_chip(1))
            n += fwd(dest, T["r" + k][:, :], T["h" + k][:, :], "r" + k)
        if t < 2 and core == _helpers(rc, dests[t + 1], topo)[2]:
            k = "x%d" % (t + 1)
            g.wait_ge(T.sem["h" + k], on_chip(1))
            n += fwd(dests[t + 1], T["b" + k][:, :], T["h" + k][:, :], "r" + k)
    if n: g.wait_ge(T.sem["sent"], n)


def rank_program(g, core, T, topo):
    rank = T.rank_of(core)
    if rank is None:
        for c in topo.cores_of(core):
            if T.rank_of(c) is not None: _relay(g, core, c, T, topo)
        return
    A = AluOpType
    COPY, RELU, SIGN = ActivationFunctionType.Copy, ActivationFunctionType.Relu, ActivationFunctionType.Sign
    eng = {"v": g.vector, "s": g.scalar, "t": g.tensor, "y": g.sync, "g": g}
    count, last_write, readers = {}, {}, {}
    known = {q: {} for q in eng}

    def settle(q, events):
        best = {}
        for s, n, snap in events:
            if known[q].get(s, 0) < n and (s not in best or best[s][0] < n): best[s] = (n, snap)
        for s in list(best):
            if any(o != s and best[o][1].get(s, 0) >= best[s][0] for o in best): del best[s]
        for s in best:
            n, snap = best[s]
            eng[q].wait_ge(T.sem[s], n)
            for k, m in list(snap.items()) + [(s, n)]: known[q][k] = max(known[q].get(k, 0), m)

    def call(q, make, reads, writes, sem=None, step=1):
        banks = [r for r in reads if r[:2] in ("pd", "pr")]
        events = []
        for r in reads: events += last_write.get(r, [])
        for r in writes + banks: events += last_write.get(r, []) + readers.get(r, [])
        settle(q, events)
        ins = make(eng[q])
        s = sem or "c" + q
        count[s] = count.get(s, 0) + step
        ins.then_inc(T.sem[s], step)
        e = (s, count[s], dict(known[q]))
        for r in reads: readers.setdefault(r, []).append(e)
        for r in writes: last_write[r], readers[r] = [e], []

    def arrived(regions, *events):
        for r in regions: last_write[r], readers[r] = [(s, n, {}) for s, n in events], []

    def load(q, dst, src, sem, writes): call(q, lambda e: e.dma_start(dst, src), [], writes, sem, 16)

    def store(q, dst, src, reads): call(q, lambda e: e.dma_start(dst, src), reads, [], "store", 16)

    def tt(out, in0, in1, op, reads, writes): call("v", lambda e: e.tensor_tensor(out, in0, in1, op), reads, writes)

    def ts(out, in0, s1, s2, op0, op1, reads, writes):
        if op1 is None: call("v", lambda e: e.tensor_scalar(out, in0, s1, None, op0), reads, writes)
        else: call("v", lambda e: e.tensor_scalar(out, in0, s1, s2, op0, op1), reads, writes)

    def vcopy(out, in_, reads, writes): call("v", lambda e: e.tensor_copy(out, in_), reads, writes)

    def scopy(out, in_, reads, writes, scale=1.0):
        if scale == 1.0: call("s", lambda e: e.activation(out, in_, COPY), reads, writes)
        else: call("s", lambda e: e.activation(out, in_, COPY, scale=scale), reads, writes)

    def scan(out, d0, d1, op0, op1, reads, writes): call("v", lambda e: e.tensor_tensor_scan(out, d0, d1, 0.0, op0, op1), reads, writes)

    def quant(q, s, in_, reads, writes): call("v", lambda e: e.quantize_mx(q, s, in_), reads, writes)

    def mm(out, lq, ls, rq, rs, reads, writes): call("t", lambda e: e.matmul_mx(out, lq, ls, rq, rs, True, True), reads, writes)

    sent = [0]
    dests = [T.cores[rank ^ s] for s in STEP]
    back = [[len(topo.engines(h, core)) for h in _helpers(d, core, topo)] for d in dests]

    def send(reads, *parts):
        settle("g", [e for r in reads for e in last_write.get(r, [])])
        if len(parts) == 1:
            h, dst, src, sem, es = parts[0]
            rid, pid = topo.addr(h, core)
            g.remote_dma(out_ap=dst, in_ap=src, remote_sem=T.sem[sem], local_sem=T.sem["sent"], pid=pid, routing_id=rid, dma_engine_mask=_mask(es))
        else:
            moves = []
            for h, dst, src, sem, es in parts:
                rid, pid = topo.addr(h, core)
                moves.append(RemoteDMATransfer(dst_ids=[DstId(rid=rid, pnc=pid)], dma_engine_mask=_mask(es), remote_sem=T.sem[sem], src=src, dst=dst))
            g.remote_dma_fused(moves, local_sem=T.sem["sent"])
        sent[0] += sum(len(p[4]) for p in parts)

    load("y", T["odi"][:, :], T.od[:, :], "lod", ["odi"])
    load("s", T["xin"][:, :], T.x[:, :], "lx", ["xin"])
    load("y", T["uin"][:, :], T.u[:, :], "lu", ["uin"])
    load("y", T["wq"][:, :].bitcast(dt.uint8), T.wc[:, :], "lwc", ["wq"])
    load("y", T["wp"][:, :], T.ws[:, :], "lws", ["wp"])
    load("y", T["vin"][:, :], T.v[:, :], "lv", ["vin"])
    ha, hb, hc = _helpers(core, dests[0], topo)
    es = topo.engines(core, ha)
    iot, ci = T["iot"], T["ci"]
    call("g", lambda e: e.iota(iot[:, :], [[1, 512]], 0, 0, allow_small_or_imprecise_dtypes=True), [], ["iot"])
    call("g", lambda e: e.iota(T["pidx"][:, :], [[1, 1]], 0, 1), [], ["pidx"])
    call("g", lambda e: e.iota(T["p4"][:, :], [[1, 4]], 0, 4, allow_small_or_imprecise_dtypes=True), [], ["p4"])
    send(["odi"], (ha, T["hod"][:, :], T["odi"][:, :], "hod", es[1::2]))
    arrived(["bi"], ("roda", back[0][0]))
    arrived(["bv"], ("rivb", back[0][1]), ("rivc", back[0][2]))
    for t in range(3):
        if t:
            arrived(["bw%d" % t], ("rw%d" % t, back[t][0]))
            arrived(["bx%d" % t], ("rx%d" % t, back[t][2]))
        arrived(["rz%d" % t], ("rqa%d" % t, back[t][0]), ("rqb%d" % t, back[t][1]), ("rs%d" % t, back[t][2]))

    ts(ci[:, :], iot[:, 0:C], -144.0, None, A.add, None, ["iot"], ["ci"])
    ts(T["p15"][:, :], T["pidx"][:, :], 15, None, A.bitwise_and, None, ["pidx"], ["p15"])
    vcopy(T["p16"][:, :], T["p15"][:, :], ["p15"], ["p16"])
    ts(T["ofc"][:, :], iot[:, 0:36], 0.0, T["p16"][:, :], A.mult, A.add, ["iot", "p16"], ["ofc"])
    ts(T["ne"][:, :], iot[:, 0:16], T["p16"][:, :], None, A.not_equal, None, ["iot", "p16"], ["ne"])
    ts(T["nx"][:, :], iot[:, 0:16], T["p16"][:, :], 1.0, A.subtract, A.is_equal, ["iot", "p16"], ["nx"])
    ts(T["t1"][:, :], T["nx"][:, :], 1048575.0, None, A.mult, None, ["nx"], ["t1"])
    tt(T["sc16"][:, :], T["t1"][:, :], T["ne"][:, :], A.add, ["t1", "ne"], ["sc16"])
    ts(T["sct"][:, :], T["p16"][:, :], 15.0, 1.0 - 2.0 ** -20, A.is_equal, A.mult, ["p16"], ["sct"])
    ts(T["scol"][:, :], T["sct"][:, :], 2.0 ** -20, None, A.add, None, ["sct"], ["scol"])
    scopy(T["scc"][:, :], T["sc16"][:, :].indirect(T["ofc"][:, :]), ["sc16", "ofc"], ["scc"])

    def wrap(src, out, writes):
        scan(T["zj"][:, :], T["scc"][:, 0:C], T[src][:, :], A.mult, A.add, ["scc", src], ["zj"])
        ts(out, T["zj"][:, 15:C:16], T["scol"][:, :], 144.25, A.mult, A.add, ["zj", "scol"], writes)

    vcopy(T["aw0"][:, 18:36], T["odi"][:, :], ["odi"], ["aw0.o"])
    vcopy(T["ivr"][:, :].indirect(T["aw0"][:, 18:36]), ci[:, :], ["ci", "aw0.o"], ["ivr"])
    wrap("ivr", T["aw0"][:, 0:18], ["aw0.i"])
    vcopy(T["ivi"][:, :], T["aw0"][:, 0:18], ["aw0.i"], ["ivi"])
    send(["ivi"], (hb, T["hiv"][:, 0:9], T["ivi"][:, 0:9], "hiv", es[0::4]), (hc, T["hiv"][:, 9:18], T["ivi"][:, 9:18], "hiv", es[2::4]))

    def off(t, k):
        return T["aw%d" % t][:, 0:18] if k == "i" else T["aw%d" % t][:, 18:36]

    def keys(t):
        tt(T["k0"][:, :], T["i5"][:, :].indirect(off(t, "i")), iot[:, 0:C], A.add, ["i5", "aw%d.i" % t, "iot"], ["k0"])

    def bank(p, b, n=C): return T[p][:, 512 * b:512 * b + n]

    def part(name, b): return T[name][:, C * b:C * b + C]

    def score(t):
        q, s = T["xq%d" % t], T["xs%d" % t]
        mm(bank("pr", 0), T["urq"][:, :], T["urp"][:, :], q[:, :], s[:, :], ["urq", "urp", "x%d" % t], ["pr0"])

    def unpack(t, b):
        q, s = T["xq%d" % t], T["xs%d" % t]
        mm(bank("pd", b), T["eq"][:, 128 * b:128 * b + 128], T["ep"][:, 128 * b:128 * b + 128], q[:, :], s[:, :], ["e", "x%d" % t], ["pd%d" % b])

    def held(b): scopy(part("fs", b), bank("pd", b), ["pd%d" % b], ["fs%d" % b])

    def signs(): call("s", lambda e: e.activation(T["fl"][:, :], bank("pr", 0), SIGN), ["pr0"], ["fl"])

    def shifted(out, in_, reads, writes): ts(out, in_, 0.25, None, A.add, None, reads, writes)

    def chase(t, mid):
        if t == 0:
            vcopy(T["b0"][:, :], T["bi"][:, :], ["bi"], ["b0"])
            scopy(T["jb"][:, :], ci[:, :].indirect(T["b0"][:, :]), ["ci", "b0"], ["jb"])
            scopy(T["ja"][:, :], T["jb"][:, :].indirect(off(0, "i")), ["jb", "aw0.i"], ["ja"])
        else:
            scopy(T["ja"][:, :], T["op%d" % t][:, :].indirect(T["bw%d" % t][:, 0:18]), ["op%d" % t, "bw%d" % t], ["ja"])
        scopy(T["c0"][:, :], T["k0"][:, :], ["k0"], ["c0"])
        wrap("ja", T["lo0"][:, :], ["lo0"])
        jr, key, twin = "ja", "k0", "c0"
        for i, r in enumerate(RAD):
            last = i == len(RAD) - 1
            lo = "lo%d" % i
            if not last:
                src = jr
                for m in range(r - 1):
                    dst = [x for x in ("ja", "jb", "jc") if x not in (src, jr)][0]
                    scopy(T[dst][:, :], T[src][:, :].indirect(T[lo][:, :]), [src, lo], [dst])
                    src = dst
            acc = key
            for m in range(r - 1):
                if last and m == r - 2: name, out = "kk0", T["kk"][:, 0:C]
                else:
                    name = [x for x in ("k0", "k1", "k2") if x not in (acc, key)][0]
                    out = T[name][:, :]
                tt(out, T[acc][:, :].indirect(T[lo][:, :]), T[twin][:, :], A.min, [acc, twin, lo], [name])
                acc = name
                if last and m == 0: mid()
            key = acc
            if not last:
                twin = "c1" if twin == "c0" else "c0"
                scopy(T[twin][:, :], T[key][:, :], [key], [twin])
                jr = src
                wrap(jr, T["lo%d" % (i + 1)][:, :], ["lo%d" % (i + 1)])

    def spread(h):
        k, a, b = str(h), C * h, C * h + C
        scan(T["zk"][:, a:b], T["dkk"][:, a:b], T["kk"][:, a:b], A.add, A.max, ["dkk", "kk" + k], ["zk" + k])

    def choose(t):
        n = t + 1
        af, aw = "af%d" % t, "aw%d" % n

        def leaders(h):
            k = str(h)
            a, b = 18 * h, 18 * h + 18
            vcopy(T["zki"][:, a:b], T["zk"][:, C * h + 15:C * h + C:16], ["zk" + k], ["zki" + k])
            ts(T["zkm"][:, a:b], T["zki"][:, a:b], 511, None, A.bitwise_and, None, ["zki" + k], ["zkm" + k])
            vcopy(T["ll"][:, a:b], T["zkm"][:, a:b], ["zkm" + k], ["ll" + k])

        def flags(h):
            k = str(h)
            call("s", lambda e: e.activation(T["tf"][:, C * h:C * h + C], T["fl"][:, :].indirect(T["ll"][:, 18 * h:18 * h + 18]), RELU), ["fl", "ll" + k], ["tf" + k])

        def take(h):
            k, r = str(h), aw + (".i", ".o")[h]
            a, b = C * h, C * h + C
            scan(T["zf"][:, a:b], T["scc"][:, a:b], T["tf"][:, a:b], A.mult, A.add, ["scc", "tf" + k], ["zf" + k])
            a, b = 18 * h, 18 * h + 18
            tt(T["fm"][:, a:b], T["zf"][:, C * h + 15:C * h + C:16], T["ds"][:, a:b], A.mult, ["zf" + k, "ds"], ["fm" + k])
            tt(T["fw"][:, a:b], T["fm"][:, a:b], T[af][:, a:b], A.add, ["fm" + k, af], ["fw" + k])
            vcopy(T[aw][:, a:b], T["fw"][:, a:b], ["fw" + k], [r])
        scopy(T["kk"][:, C:2 * C], T["kk"][:, 0:C].indirect(off(t, "o")), ["kk0", "aw%d.o" % t], ["kk1"])
        leaders(0)
        signs()
        if t == 0:
            shifted(T["bf"][:, 0:18], T["bv"][:, :], ["bv"], ["bf.i"])
            shifted(T["bf"][:, 18:36], T["bi"][:, :], ["bi"], ["bf.o"])
        else:
            shifted(T["bf"][:, 0:18], T["bw%d" % t][:, :], ["bw%d" % t], ["bf.i"])
            shifted(T["bf"][:, 18:36], T["bx%d" % t][:, :], ["bx%d" % t], ["bf.o"])
        tt(T["df"][:, :], T["bf"][:, :], T[af][:, :], A.subtract, ["bf.i", "bf.o", af], ["df"])
        ts(T["ds"][:, :], T["df"][:, :], T["scol"][:, :], None, A.mult, None, ["df", "scol"], ["ds"])
        flags(0)
        spread(1)
        leaders(1)
        if t: held(0)
        flags(1)
        take(0)
        if n < 3: send([aw + ".i"], (_helpers(core, dests[n], topo)[0], T["hw%d" % n][:, :], T[aw][:, 0:18], "hw%d" % n, es))
        take(1)
        if t:
            for b in (1, 2): held(b)

    def means(t):
        n = t + 1
        o, ro = off(n, "o"), "aw%d.o" % n

        def pair(b): tt(part("ys", b), part("gs", b), bank("pd", b), A.add, ["gs%d" % b, "pd%d" % b], ["ys%d" % b])
        for b in (1, 2, 3):
            scopy(part("gs", b), part("fs", b).indirect(o), ["fs%d" % b, ro], ["gs%d" % b])
            if t and b == 1: held(3)
        vcopy(part("gs", 0), part("fs", 0).indirect(o), ["fs0", ro], ["gs0"])
        for k, b in ("y1", "y0", "z1", "y2", "y3", "z2"):
            b = int(b)
            if k == "y": pair(b)
            else: ts(T["zt"][:, b:4 * C:4], part("ys", b).indirect(o), 0.5, None, A.mult, None, ["ys%d" % b, ro], ["zt%d" % b])
        for b in (0, 3): scopy(T["zt"][:, b:4 * C:4], part("ys", b).indirect(o), ["ys%d" % b, ro], ["zt%d" % b], 0.5)
        zq, zs = T["zq%d" % t], T["zs%d" % t]
        quant(zq[:, :], zs[:, :], T["zt"][:, :], ["zt0", "zt1", "zt2", "zt3"], ["z%d" % t])
        a, b, c = _helpers(core, dests[t], topo)
        hq, h = T["hq%d" % t], C // 2
        send(["z%d" % t], (a, hq[:, 0:h].bitcast(dt.uint8), zq[:, 0:h].bitcast(dt.uint8), "hq%d" % t, es[1::2]),
             (b, hq[:, h:C].bitcast(dt.uint8), zq[:, h:C].bitcast(dt.uint8), "hq%d" % t, es[0::2]))
        send(["z%d" % t], (c, T["hs%d" % t][:, :], zs[:, :], "hs%d" % t, es))
        if n < 3:
            send([ro], (_helpers(core, dests[n], topo)[2], T["hx%d" % n][:, :], o, "hx%d" % n, es))
            scopy(T["op%d" % n][:, :], ci[:, :].indirect(o), ["ci", ro], ["op%d" % n])
            keys(n)
            shifted(T["af%d" % n][:, :], T["aw%d" % n][:, :], ["aw%d.i" % n, "aw%d.o" % n], ["af%d" % n])
        for b in SUMMED: scopy(part("fp", b), part("fs", b).indirect(o), ["fs%d" % b, ro], ["fp%d" % b], 32.0)

    def products(t):
        n = t + 1
        i, ri = off(n, "i"), "aw%d.i" % n
        rq, rs = T["rq%d" % t], T["rs%d" % t]
        for b in range(4):
            mm(bank("pr", b), T["wq"][:, 128 * b:128 * b + 128], T["wp"][:, 128 * b:128 * b + 128], rq[:, :], rs[:, :], ["wq", "wp", "rz%d" % t], ["pr%d" % b])
        for b in SUMMED: tt(part("rr", b), bank("pr", b), part("fp", b), A.add, ["pr%d" % b, "fp%d" % b], ["rr%d" % b])

        def scaled(b): scopy(part("rr", b), bank("pr", b), ["pr%d" % b], ["rr%d" % b], 0.03125)

        def moved(b): scopy(T["xt"][:, b:4 * C:4], part("rr", b).indirect(i), ["rr%d" % b, ri], ["xt%d" % b], 0.03125)
        for f, b in ((scaled, 1), (moved, 0), (scaled, 3), (moved, 2)): f(b)

    def state(t):
        n = t + 1
        i, ri = off(n, "i"), "aw%d.i" % n
        for b in range(4):
            if b not in SUMMED: tt(T["xt"][:, b:4 * C:4], part("rr", b).indirect(i), part("fs", b), A.add, ["rr%d" % b, ri, "fs%d" % b], ["xt%d" % b])
        if n < 3: spread(0)
        quant(T["xq%d" % n][:, :], T["xs%d" % n][:, :], T["xt"][:, :], ["xt0", "xt1", "xt2", "xt3"], ["x%d" % n])
        if n < 3:
            score(n)
            for b in range(4): unpack(n, b)

    ts(T["t1"][:, :], T["ne"][:, :], 1.0, 2.0 ** 20, A.subtract, A.mult, ["ne"], ["t1"])
    ts(T["t2"][:, :], T["nx"][:, :], 2.0 ** 18, None, A.mult, None, ["nx"], ["t2"])
    tt(T["dk16"][:, :], T["t1"][:, :], T["t2"][:, :], A.add, ["t1", "t2"], ["dk16"])
    scopy(T["dkk"][:, :], T["dk16"][:, :].indirect(T["ofc"][:, :]), ["dk16", "ofc"], ["dkk"])
    ts(T["i5"][:, :], iot[:, 0:C], 512.0, None, A.mult, None, ["iot"], ["i5"])
    keys(0)
    ts(T["uof"][:, :], iot[:, 0:8], 16.0, None, A.mult, None, ["iot"], ["uof"])
    for b in range(4): ts(T["et"][:, 512 * b:512 * b + 512], iot[:, :], T["p4"][:, b:b + 1], None, A.is_equal, None, ["iot", "p4"], ["et%d" % b])
    quant(T["eq"][:, :], T["ep"][:, :], T["et"][:, :], ["et0", "et1", "et2", "et3"], ["e"])
    quant(T["xq0"][:, :], T["xs0"][:, :], T["xin"][:, :], ["xin"], ["x0"])
    for b in range(4): unpack(0, b)
    for b in range(4): held(b)
    quant(T["uq"][:, :], T["up"][:, :], T["uin"][:, :], ["uin"], ["u"])
    vcopy(T["urq"][:, :].bitcast(dt.uint32), T["uq"][:, :].bitcast(dt.uint32).indirect(T["uof"][:, :]), ["u", "uof"], ["urq"])
    vcopy(T["urp"][:, :], T["up"][:, :].indirect(T["uof"][:, :]), ["u", "uof"], ["urp"])
    score(0)
    shifted(T["af0"][:, :], T["aw0"][:, :], ["aw0.i", "aw0.o"], ["af0"])
    chase(0, lambda: None)
    spread(0)
    choose(0)
    means(0)
    for t in (1, 2):
        chase(t, lambda: products(t - 1))
        state(t - 1)
        choose(t)
        means(t)
    quant(T["vq"][:, :], T["vp"][:, :], T["vin"][:, :], ["vin"], ["v"])
    vcopy(T["fr"][:, :], iot[:, 0:C].indirect(off(3, "o")), ["iot", "aw3.o"], ["fr"])
    for k in range(8): store("y", T.fo[k:k + 1, :], T["fr"][16 * k:16 * k + 1, :], ["fr"])
    products(2)
    state(2)
    store("y", T.oc[:, :], T["xq3"][:, :].bitcast(dt.uint8), ["x3"])
    h = C // 2
    for k in range(2): mm(bank("pr", k, h), T["vq"][:, :], T["vp"][:, :], T["xq3"][:, h * k:h * k + h], T["xs3"][:, h * k:h * k + h], ["v", "x3"], ["pr%d" % k])
    for k in range(4): store("y" if k < 2 else "s", T.osc[4 * k:4 * k + 4, :], T["xs3"][32 * k:32 * k + 4, :], ["x3"])
    vcopy(T["yo"][:, 0:h], bank("pr", 0, h), ["pr0"], ["yo0"])
    scopy(T["yo"][:, h:C], bank("pr", 1, h), ["pr1"], ["yo1"])
    store("y", T.y[:, 0:h], T["yo"][:, 0:h], ["yo0"])
    store("s", T.y[:, h:C], T["yo"][:, h:C], ["yo1"])
    for s in ("cv", "cs", "ct", "cg", "store"): g.wait_ge(T.sem[s], count[s])
    g.wait_ge(T.sem["sent"], sent[0])
